import numpy as np
import ml_dtypes


def mxq(x, axis, fmt="e4m3"):
    dtype, down = {"e4m3": (ml_dtypes.float8_e4m3fn, 7), "e5m2": (ml_dtypes.float8_e5m2, 14)}[fmt]
    v = np.moveaxis(np.asarray(x, np.float32).astype(ml_dtypes.bfloat16).astype(np.float64), axis, -1)
    blocks = v.reshape(v.shape[:-1] + (-1, 32))
    amax = np.abs(blocks).max(-1, keepdims=True)
    byte = np.maximum(np.where(amax > 0, np.frexp(amax)[1] - 1 + 127, 0) - down, 1)
    scale = np.exp2(byte - 127.0)
    codes = (blocks / scale).astype(np.float32).astype(dtype).astype(np.float64)
    return np.moveaxis((codes * scale).reshape(v.shape), -1, axis)


WIDE = False


def mx_kscale(k):
    if not WIDE:
        return np.ones(k)
    levels = np.array([10, -10, 5, -5, 0])
    if k % 512:
        return np.exp2(np.random.permutation(np.resize(levels, k // 32))).repeat(32)
    a = np.empty((k // 512, 16))
    for p in range(k // 512):
        a[p, :8] = np.random.permutation(np.resize(levels, 8))
        for g in range(8):
            far = levels[np.abs(levels - a[p, g]) >= 10]
            a[p, g + 8] = far[np.random.randint(len(far))]
    return np.exp2(a.ravel()).repeat(32)


def f64(x):
    return np.asarray(x).astype(np.float64)


def striped(idx):
    return np.tile(idx.reshape(-1, 16).T, (8, 1)).astype(np.uint16)


def unstriped(offs):
    return offs[:16].T.reshape(-1).astype(np.int64)


def striped8(idx):
    return np.concatenate([x.reshape(-1, 16).T for x in idx]).astype(np.uint16)


def runs(offs, k):
    lists = np.stack([offs[16 * r : 16 * r + 16].T.reshape(-1) for r in range(8)]).astype(np.int64)
    return lists[np.arange(k) % 512 // 64]


def pack_weight(w):
    k, n = w.shape
    w = f64(np.asarray(w, np.float32).astype(ml_dtypes.bfloat16)).reshape(k // 32, 32, n)
    amax = np.abs(w).max(1)
    byte = np.clip(np.where(amax > 0, np.frexp(amax)[1] - 1 + 127 - 7, 1), 1, 254)
    scaled = (w * np.exp2(127.0 - byte)[:, None, :]).reshape(k, n).astype(np.float32)
    words = np.ascontiguousarray(scaled.reshape(k // 512, 128, 4, n).transpose(0, 1, 3, 2)).astype(ml_dtypes.float8_e4m3fn).view(np.uint8)
    return words, np.ascontiguousarray(byte.astype(np.uint8).reshape(k // 512, 16, n))


def unpack_weight(words, scales):
    g, p, n, _ = words.shape
    vals = np.ascontiguousarray(words).view(ml_dtypes.float8_e4m3fn).astype(np.float64) * np.repeat(np.exp2(scales.astype(np.float64) - 127.0), 8, axis=1)[..., None]
    return vals.transpose(0, 1, 3, 2).reshape(g * 512, n)


def sigmoid(v):
    return 1.0 / (1.0 + np.exp(-np.maximum(v, -700.0)))

def planes(y):
    n, m = y.shape
    v = y.astype(np.float32).astype(ml_dtypes.bfloat16).astype(np.float64).reshape(n // 32, 32, m)
    top = np.abs(v).max(1)
    byte = np.clip(np.where(top > 0, np.frexp(top)[1] - 1 + 127 - 7, 1), 1, 254)
    codes = (v * np.exp2(127.0 - byte)[:, None, :]).reshape(n, m).astype(np.float32).astype(ml_dtypes.float8_e4m3fn).view(np.uint8)
    words = codes.reshape(n // 512, 128, 4, m).transpose(0, 1, 3, 2)
    return np.ascontiguousarray(words), np.ascontiguousarray(byte.astype(np.uint8).reshape(n // 512, 16, m))


K, T, S, N, H = 512, 2048, 512, 512, 512


def setup_inputs():
    n = np.random.standard_normal
    s = mx_kscale(K)[:, None]
    u = mx_kscale(H)
    packed_xT = pack_weight(n((K, T)) * s)
    packed_w1 = pack_weight(n((K, H)) / np.sqrt(K) / s)
    packed_w2 = pack_weight(n((H, N)) / np.sqrt(2 * H) / u[:, None])
    packed_w3 = pack_weight(n((K, N)) / np.sqrt(2 * K) / s)
    return {
        "x_words": packed_xT[0],
        "x_scales": packed_xT[1],
        "w1_words": packed_w1[0],
        "w1_scales": packed_w1[1],
        "gn": (np.random.uniform(0.5, 1.5, (H, 1)) * u[:, None]).astype(np.float32),
        "w2_words": packed_w2[0],
        "w2_scales": packed_w2[1],
        "w3_words": packed_w3[0],
        "w3_scales": packed_w3[1],
        "sl": np.random.uniform(1.0, 2.0, (N, 1)).astype(np.float32),
        "offs": striped(np.random.permutation(T)[:S]),
        "n1": striped8(np.stack([np.random.permutation(S) for _ in range(8)])),
        "two": striped(np.random.permutation(T)[:S]),
        "n2": striped(np.random.permutation(S)),
    }


def reference(x_words, x_scales, w1_words, w1_scales, gn, w2_words, w2_scales, w3_words, w3_scales, sl, offs, n1, two, n2):
    xq = unpack_weight(x_words, x_scales)[:, unstriped(offs)]
    y = unpack_weight(w1_words, w1_scales).T @ xq
    z = f64(gn) * (y - (y[np.arange(H)[:, None], runs(n1, H)]))
    x_two = unpack_weight(x_words, x_scales)[:, unstriped(two)]
    h = unpack_weight(w2_words, w2_scales).T @ mxq(z, 0, "e4m3") + unpack_weight(w3_words, w3_scales).T @ x_two
    mu = h.mean(axis=1, keepdims=True)
    sg = sigmoid(f64(sl) * (h[:, unstriped(n2)] - mu))
    out_0 = (h - mu) * sg
    return (out_0,) + planes(out_0)

@@ -1,0 +1,215 @@
+from contextlib import ExitStack
+
+import concourse.mybir as mybir
+
+K, T, S, N, H = 512, 2048, 512, 512, 512
+FLOPS = 2 * S * (K * H + H * N + K * N)
+
+F32 = mybir.dt.float32
+BF16 = mybir.dt.bfloat16
+I32 = mybir.dt.int32
+U32 = mybir.dt.uint32
+U16 = mybir.dt.uint16
+U8 = mybir.dt.uint8
+FP8X4 = mybir.dt.float8_e4m3fn_x4
+ALU = mybir.AluOpType
+ACT = mybir.ActivationFunctionType
+
+P = 128
+PACK = 4
+QUADS = 4
+LIST_ROWS = 16
+HALF = S // 2
+Z_CHUNKS = (256, 256)
+OUT_CHUNKS = (256, 128, 128)
+
+
+def tile_picked_mixindifecn_none_po_kernel(
+    tc, x_words, x_scales, w1_words, w1_scales, gn, w2_words, w2_scales, w3_words, w3_scales, sl, offs, n1, two, n2,
+    out_0, out_1, out_2,
+):
+    nc = tc.nc
+
+    def as_words(dram):
+        return dram[0].rearrange("p n t -> p (n t)").bitcast(I32)
+
+    def load_scale_rows(queues, plane, dram):
+        rows = dram[0].bitcast(I32)
+        for q, queue in enumerate(queues):
+            top = 32 * q
+            queue.dma_start(out=plane[top : top + 4, :].bitcast(I32), in_=rows[4 * q : 4 * q + 4, :])
+
+    def entries(lists, start, width):
+        return lists[:, start // LIST_ROWS : (start + width) // LIST_ROWS]
+
+    def dealt(tile):
+        return tile[:].rearrange("p (t m) -> p m t", t=PACK)
+
+    def in_order(ap):
+        return ap.rearrange("p (m t) -> p m t", t=PACK)
+
+    def deal_on_gpsimd(dst, src):
+        nc.gpsimd.tensor_copy(dst.rearrange("p (t m) -> p t m", t=PACK), src.rearrange("p (m t) -> p t m", t=PACK))
+
+    with ExitStack() as ctx:
+        sb = ctx.enter_context(tc.tile_pool(name="sb", bufs=1))
+        ps = ctx.enter_context(tc.psum_pool(name="ps", bufs=1))
+
+        offs_t = sb.tile([P, S // LIST_ROWS], U16, name="offs_t")
+        two_t = sb.tile([P, S // LIST_ROWS], U16, name="two_t")
+        n1_t = sb.tile([P, S // LIST_ROWS], U16, name="n1_t")
+        n2_t = sb.tile([P, S // LIST_ROWS], U16, name="n2_t")
+        xw = sb.tile([P, T], I32, name="xw", align_bytes=64)
+        xs = sb.tile([P, T], U8, name="xs", align_bytes=64)
+        w1_raw = sb.tile([P, H], I32, name="w1_raw", align_bytes=64)
+        w2_raw = sb.tile([P, N], I32, name="w2_raw", align_bytes=64)
+        w3_raw = sb.tile([P, N], I32, name="w3_raw", align_bytes=64)
+        s1_raw = sb.tile([P, H], U8, name="s1_raw", align_bytes=64)
+        s2_raw = sb.tile([P, N], U8, name="s2_raw", align_bytes=64)
+        s3_raw = sb.tile([P, N], U8, name="s3_raw", align_bytes=64)
+        w1 = sb.tile([P, H], U32, name="w1", align_bytes=64)
+        w2 = sb.tile([P, N], U32, name="w2", align_bytes=64)
+        w3 = sb.tile([P, N], U32, name="w3", align_bytes=64)
+        s1 = sb.tile([P, H], U8, name="s1", align_bytes=64)
+        s2 = sb.tile([P, N], U8, name="s2", align_bytes=64)
+        s3 = sb.tile([P, N], U8, name="s3", align_bytes=64)
+        gain = sb.tile([P, PACK], F32, name="gain")
+        slope = sb.tile([P, PACK], F32, name="slope")
+        coef = sb.tile([P, PACK, 2], F32, name="coef")
+
+        nc.gpsimd.memset(xs[:].bitcast(I32), 0)
+        nc.vector.memset(s1_raw[:].bitcast(I32), 0)
+        nc.vector.memset(s3_raw[:].bitcast(I32), 0)
+        nc.vector.memset(s2_raw[:].bitcast(I32), 0)
+        nc.vector.memset(coef[:], -1.0 / S)
+
+        nc.sync.dma_start(offs_t[:], offs)
+        nc.scalar.dma_start(out=gain[:], in_=gn.rearrange("(p t) o -> p (t o)", t=PACK))
+        nc.sync.dma_start(two_t[:], two)
+        nc.sync.dma_start(out=xw[:], in_=as_words(x_words))
+        load_scale_rows([nc.scalar] * QUADS, xs, x_scales)
+        load_scale_rows([nc.scalar, nc.scalar, nc.gpsimd, nc.gpsimd], s1_raw, w1_scales)
+        nc.sync.dma_start(out=w1_raw[:], in_=as_words(w1_words))
+        nc.sync.dma_start(out=slope[:], in_=sl.rearrange("(p t) o -> p (t o)", t=PACK))
+        nc.sync.dma_start(n1_t[:], n1)
+        nc.sync.dma_start(out=w3_raw[:], in_=as_words(w3_words))
+        load_scale_rows([nc.sync] * QUADS, s3_raw, w3_scales)
+        nc.sync.dma_start(out=w2_raw[:], in_=as_words(w2_words))
+        load_scale_rows([nc.sync] * QUADS, s2_raw, w2_scales)
+        nc.sync.dma_start(n2_t[:], n2)
+
+        nc.scalar.activation(coef[:, :, 0], slope[:], ACT.Copy, scale=-1.0 / S)
+
+        a_scales = sb.tile([P, S], U8, name="a_scales", align_bytes=64)
+        b_scales = sb.tile([P, S], U8, name="b_scales", align_bytes=64)
+        a_words = [sb.tile([P, HALF], U32, name=f"a_words{u}", align_bytes=64) for u in range(2)]
+        b_words = sb.tile([P, S], U32, name="b_words", align_bytes=64)
+        nc.vector.tensor_copy(a_scales[:], xs[:].indirect(offs_t[:]))
+        deal_on_gpsimd(s1[:], s1_raw[:])
+        nc.vector.tensor_copy(b_scales[:], xs[:].indirect(two_t[:]))
+        nc.scalar.copy(dealt(w1), in_order(w1_raw[:].bitcast(U32)))
+        for u in range(2):
+            nc.vector.tensor_copy(a_words[u][:], xw[:].bitcast(U32).indirect(entries(offs_t, u * HALF, HALF)))
+        nc.vector.tensor_copy(b_words[:], xw[:].bitcast(U32).indirect(two_t[:]))
+        deal_on_gpsimd(w3[:], w3_raw[:].bitcast(U32))
+        deal_on_gpsimd(s3[:], s3_raw[:])
+        deal_on_gpsimd(w2[:], w2_raw[:].bitcast(U32))
+        deal_on_gpsimd(s2[:], s2_raw[:])
+
+        y_ps = [ps.tile([P, S], F32, name=f"y_ps{t}") for t in range(PACK)]
+        h_ps = [ps.tile([P, S], F32, name=f"h_ps{t}") for t in range(PACK)]
+        for pair in range(2):
+            for u in range(2):
+                for t in (2 * pair, 2 * pair + 1):
+                    m = slice(t * P, (t + 1) * P)
+                    cols = slice(u * HALF, (u + 1) * HALF)
+                    nc.tensor.matmul_mx(
+                        out=y_ps[t][:, cols], lhsT=w1[:, m].bitcast(FP8X4), lhsT_scale=s1[:, m],
+                        rhs=a_words[u][:].bitcast(FP8X4), rhs_scale=a_scales[:, cols], start=True, stop=True,
+                    )
+        for t in range(PACK):
+            m = slice(t * P, (t + 1) * P)
+            nc.tensor.matmul_mx(
+                out=h_ps[t][:], lhsT=w3[:, m].bitcast(FP8X4), lhsT_scale=s3[:, m],
+                rhs=b_words[:].bitcast(FP8X4), rhs_scale=b_scales[:], start=True, stop=False,
+            )
+
+        y_win = [sb.tile([P, S], F32, name=f"y_win{t}", align_bytes=64) for t in range(PACK)]
+        for t in range(PACK):
+            nc.scalar.activation(y_win[t][:], y_ps[t][:], ACT.Copy, scale=gain[:, t : t + 1])
+
+        start = 0
+        for c, width in enumerate(Z_CHUNKS):
+            cols = slice(start, start + width)
+            other = [sb.tile([P, width], F32, name=f"other{c}_{t}", align_bytes=64) for t in range(PACK)]
+            z_rows = sb.tile([P, PACK, width], BF16, name=f"z_rows{c}", align_bytes=64)
+            z_side = sb.tile([P, width * PACK], BF16, name=f"z_side{c}", align_bytes=64)
+            z_words = sb.tile([P, width], U32, name=f"z_words{c}", align_bytes=64)
+            z_scales = sb.tile([P, width], U8, name=f"z_scales{c}", align_bytes=64)
+            for t in range(PACK):
+                looked_up = y_win[t][:].indirect(entries(n1_t, start, width))
+                if c == 0 and t < 2:
+                    nc.vector.tensor_copy(other[t][:], looked_up)
+                else:
+                    nc.scalar.activation(other[t][:], looked_up, ACT.Copy)
+            for t in range(PACK):
+                nc.vector.scalar_tensor_tensor(
+                    out=z_rows[:, t, :], in0=y_ps[t][:, cols], scalar=gain[:, t : t + 1], in1=other[t][:],
+                    op0=ALU.mult, op1=ALU.subtract,
+                )
+            nc.vector.tensor_copy(
+                z_side[:].rearrange("p (c i t) -> p c t i", i=4, t=PACK),
+                z_rows[:].rearrange("p t (c i) -> p c t i", i=4),
+            )
+            nc.vector.quantize_mx(out=z_words[:].bitcast(FP8X4), scales=z_scales[:], in_=z_side[:])
+            for t in range(PACK):
+                m = slice(t * P, (t + 1) * P)
+                nc.tensor.matmul_mx(
+                    out=h_ps[t][:, cols], lhsT=w2[:, m].bitcast(FP8X4), lhsT_scale=s2[:, m],
+                    rhs=z_words[:].bitcast(FP8X4), rhs_scale=z_scales[:], start=False, stop=(c == len(Z_CHUNKS) - 1),
+                )
+            start += width
+
+        h_win = [sb.tile([P, S], F32, name=f"h_win{t}", align_bytes=64) for t in range(PACK)]
+        h_sum = [sb.tile([P, 1], F32, name=f"h_sum{t}") for t in range(PACK)]
+        shift = [sb.tile([P, 2], F32, name=f"shift{t}") for t in range(PACK)]
+        for t in range(PACK):
+            nc.vector.tensor_scalar(
+                out=h_win[t][:], in0=h_ps[t][:], scalar1=1.0, scalar2=None, op0=ALU.mult, op1=ALU.add,
+                accum_out=h_sum[t][:],
+            )
+            nc.vector.tensor_scalar(
+                out=shift[t][:], in0=coef[:, t, :], scalar1=h_sum[t][:], scalar2=None, op0=ALU.mult,
+            )
+
+        out_rows = out_0.rearrange("(p t) n -> p t n", t=PACK)
+        out_words = as_words(out_1)
+        o_scales = sb.tile([P, S], U8, name="o_scales", align_bytes=64)
+        start = 0
+        for c, width in enumerate(OUT_CHUNKS):
+            cols = slice(start, start + width)
+            gate = [sb.tile([P, width], F32, name=f"gate{c}_{t}", align_bytes=64) for t in range(PACK)]
+            o_rows = sb.tile([P, PACK, width], F32, name=f"o_rows{c}", align_bytes=64)
+            o_side = sb.tile([P, width * PACK], BF16, name=f"o_side{c}", align_bytes=64)
+            o_words = sb.tile([P, width], I32, name=f"o_words{c}", align_bytes=64)
+            for t in range(PACK):
+                nc.scalar.activation(
+                    gate[t][:], h_win[t][:].indirect(entries(n2_t, start, width)), ACT.Sigmoid,
+                    bias=shift[t][:, 0:1], scale=slope[:, t : t + 1],
+                )
+                nc.vector.scalar_tensor_tensor(
+                    out=o_rows[:, t, :], in0=h_ps[t][:, cols], scalar=shift[t][:, 1:2], in1=gate[t][:],
+                    op0=ALU.add, op1=ALU.mult,
+                )
+            nc.sync.dma_start(out=out_rows[:, :, cols], in_=o_rows[:])
+            nc.vector.tensor_copy(
+                o_side[:].rearrange("p (c i t) -> p c t i", i=4, t=PACK),
+                o_rows[:].rearrange("p t (c i) -> p c t i", i=4),
+            )
+            nc.vector.quantize_mx(out=o_words[:].bitcast(FP8X4), scales=o_scales[:, cols], in_=o_side[:])
+            nc.sync.dma_start(out=out_words[:, cols], in_=o_words[:])
+            start += width
+        scale_rows = out_2[0].bitcast(I32)
+        for q in range(QUADS):
+            queue = nc.scalar if q % 2 else nc.sync
+            queue.dma_start(out=scale_rows[4 * q : 4 * q + 4, :], in_=o_scales[32 * q : 32 * q + 4, :].bitcast(I32))

@@ -20,7 +20,7 @@ PACK = 4
 QUADS = 4
 LIST_ROWS = 16
 HALF = S // 2
-Z_CHUNKS = (256, 256)
+Z_CHUNKS = (256, 128, 128)
 OUT_CHUNKS = (256, 128, 128)
 
 
@@ -33,23 +33,20 @@ def tile_picked_mixindifecn_none_po_kernel(
     def as_words(dram):
         return dram[0].rearrange("p n t -> p (n t)").bitcast(I32)
 
-    def load_scale_rows(queues, plane, dram):
+    def load_scale_rows(queues, plane, first_row, dram):
         rows = dram[0].bitcast(I32)
         for q, queue in enumerate(queues):
-            top = 32 * q
+            top = 32 * q + first_row
             queue.dma_start(out=plane[top : top + 4, :].bitcast(I32), in_=rows[4 * q : 4 * q + 4, :])
 
     def entries(lists, start, width):
         return lists[:, start // LIST_ROWS : (start + width) // LIST_ROWS]
 
-    def dealt(tile):
-        return tile[:].rearrange("p (t m) -> p m t", t=PACK)
+    def deal(copy, dst, src):
+        copy(dst.rearrange("p (t m) -> p m t", t=PACK), src.rearrange("p (m t) -> p m t", t=PACK))
 
-    def in_order(ap):
-        return ap.rearrange("p (m t) -> p m t", t=PACK)
-
-    def deal_on_gpsimd(dst, src):
-        nc.gpsimd.tensor_copy(dst.rearrange("p (t m) -> p t m", t=PACK), src.rearrange("p (m t) -> p t m", t=PACK))
+    def side_by_side(copy, dst, src):
+        copy(dst.rearrange("p (c i t) -> p c t i", i=4, t=PACK), src.rearrange("p t (c i) -> p c t i", i=4))
 
     with ExitStack() as ctx:
         sb = ctx.enter_context(tc.tile_pool(name="sb", bufs=1))
@@ -64,60 +61,57 @@ def tile_picked_mixindifecn_none_po_kernel(
         w1_raw = sb.tile([P, H], I32, name="w1_raw", align_bytes=64)
         w2_raw = sb.tile([P, N], I32, name="w2_raw", align_bytes=64)
         w3_raw = sb.tile([P, N], I32, name="w3_raw", align_bytes=64)
-        s1_raw = sb.tile([P, H], U8, name="s1_raw", align_bytes=64)
-        s2_raw = sb.tile([P, N], U8, name="s2_raw", align_bytes=64)
-        s3_raw = sb.tile([P, N], U8, name="s3_raw", align_bytes=64)
+        s1_raw = sb.tile([P, H], U8, name="s1_raw", tag="s1_then_a", align_bytes=64)
+        s32_raw = sb.tile([P, N], U8, name="s32_raw", align_bytes=64)
         w1 = sb.tile([P, H], U32, name="w1", align_bytes=64)
         w2 = sb.tile([P, N], U32, name="w2", align_bytes=64)
         w3 = sb.tile([P, N], U32, name="w3", align_bytes=64)
         s1 = sb.tile([P, H], U8, name="s1", align_bytes=64)
-        s2 = sb.tile([P, N], U8, name="s2", align_bytes=64)
-        s3 = sb.tile([P, N], U8, name="s3", align_bytes=64)
+        s32 = sb.tile([P, N], U8, name="s32", align_bytes=64)
         gain = sb.tile([P, PACK], F32, name="gain")
         slope = sb.tile([P, PACK], F32, name="slope")
         coef = sb.tile([P, PACK, 2], F32, name="coef")
 
-        nc.gpsimd.memset(xs[:].bitcast(I32), 0)
-        nc.vector.memset(s1_raw[:].bitcast(I32), 0)
-        nc.vector.memset(s3_raw[:].bitcast(I32), 0)
-        nc.vector.memset(s2_raw[:].bitcast(I32), 0)
+        nc.vector.memset(xs[:].bitcast(I32), 0)
         nc.vector.memset(coef[:], -1.0 / S)
+        nc.vector.memset(s1_raw[:].bitcast(I32), 0)
+        nc.vector.memset(s32_raw[:].bitcast(I32), 0)
 
         nc.sync.dma_start(offs_t[:], offs)
-        nc.scalar.dma_start(out=gain[:], in_=gn.rearrange("(p t) o -> p (t o)", t=PACK))
+        nc.scalar.dma_start(out=slope[:], in_=sl.rearrange("(p t) o -> p (t o)", t=PACK))
         nc.sync.dma_start(two_t[:], two)
+        load_scale_rows([nc.sync] * QUADS, xs, 0, x_scales)
         nc.sync.dma_start(out=xw[:], in_=as_words(x_words))
-        load_scale_rows([nc.scalar] * QUADS, xs, x_scales)
-        load_scale_rows([nc.scalar, nc.scalar, nc.gpsimd, nc.gpsimd], s1_raw, w1_scales)
+        load_scale_rows([nc.sync] * QUADS, s1_raw, 0, w1_scales)
+        nc.gpsimd.dma_start(out=gain[:], in_=gn.rearrange("(p t) o -> p (t o)", t=PACK))
         nc.sync.dma_start(out=w1_raw[:], in_=as_words(w1_words))
-        nc.sync.dma_start(out=slope[:], in_=sl.rearrange("(p t) o -> p (t o)", t=PACK))
-        nc.sync.dma_start(n1_t[:], n1)
         nc.sync.dma_start(out=w3_raw[:], in_=as_words(w3_words))
-        load_scale_rows([nc.sync] * QUADS, s3_raw, w3_scales)
         nc.sync.dma_start(out=w2_raw[:], in_=as_words(w2_words))
-        load_scale_rows([nc.sync] * QUADS, s2_raw, w2_scales)
+        load_scale_rows([nc.sync] * QUADS, s32_raw, 0, w3_scales)
+        load_scale_rows([nc.sync, nc.sync, nc.gpsimd, nc.gpsimd], s32_raw, 4, w2_scales)
+        nc.sync.dma_start(n1_t[:], n1)
         nc.sync.dma_start(n2_t[:], n2)
 
         nc.scalar.activation(coef[:, :, 0], slope[:], ACT.Copy, scale=-1.0 / S)
 
         a_scales = sb.tile([P, S], U8, name="a_scales", align_bytes=64)
         b_scales = sb.tile([P, S], U8, name="b_scales", align_bytes=64)
-        a_words = [sb.tile([P, HALF], U32, name=f"a_words{u}", align_bytes=64) for u in range(2)]
-        b_words = sb.tile([P, S], U32, name="b_words", align_bytes=64)
+        picked = sb.tile([P, 2 * S], U32, name="picked", tag="s1_then_a", align_bytes=64)
+        a_words = picked[:, 0:S]
+        b_words = picked[:, S : 2 * S]
         nc.vector.tensor_copy(a_scales[:], xs[:].indirect(offs_t[:]))
-        deal_on_gpsimd(s1[:], s1_raw[:])
         nc.vector.tensor_copy(b_scales[:], xs[:].indirect(two_t[:]))
-        nc.scalar.copy(dealt(w1), in_order(w1_raw[:].bitcast(U32)))
+        deal(nc.vector.tensor_copy, s1[:], s1_raw[:])
+        deal(nc.scalar.copy, w1[:], w1_raw[:].bitcast(U32))
         for u in range(2):
-            nc.vector.tensor_copy(a_words[u][:], xw[:].bitcast(U32).indirect(entries(offs_t, u * HALF, HALF)))
-        nc.vector.tensor_copy(b_words[:], xw[:].bitcast(U32).indirect(two_t[:]))
-        deal_on_gpsimd(w3[:], w3_raw[:].bitcast(U32))
-        deal_on_gpsimd(s3[:], s3_raw[:])
-        deal_on_gpsimd(w2[:], w2_raw[:].bitcast(U32))
-        deal_on_gpsimd(s2[:], s2_raw[:])
+            nc.vector.tensor_copy(a_words[:, u * HALF : (u + 1) * HALF], xw[:].bitcast(U32).indirect(entries(offs_t, u * HALF, HALF)))
+        deal(nc.scalar.copy, w3[:], w3_raw[:].bitcast(U32))
+        nc.vector.tensor_copy(b_words, xw[:].bitcast(U32).indirect(two_t[:]))
+        deal(nc.vector.tensor_copy, w2[:].bitcast(I32), w2_raw[:])
+        deal(nc.vector.tensor_copy, s32[:], s32_raw[:])
 
         y_ps = [ps.tile([P, S], F32, name=f"y_ps{t}") for t in range(PACK)]
-        h_ps = [ps.tile([P, S], F32, name=f"h_ps{t}") for t in range(PACK)]
+        h_ps = [[ps.tile([P, 2, HALF], F32, name=f"h_ps{u}_{pair}") for pair in range(2)] for u in range(2)]
         for pair in range(2):
             for u in range(2):
                 for t in (2 * pair, 2 * pair + 1):
@@ -125,22 +119,30 @@ def tile_picked_mixindifecn_none_po_kernel(
                     cols = slice(u * HALF, (u + 1) * HALF)
                     nc.tensor.matmul_mx(
                         out=y_ps[t][:, cols], lhsT=w1[:, m].bitcast(FP8X4), lhsT_scale=s1[:, m],
-                        rhs=a_words[u][:].bitcast(FP8X4), rhs_scale=a_scales[:, cols], start=True, stop=True,
+                        rhs=a_words[:, cols].bitcast(FP8X4), rhs_scale=a_scales[:, cols], start=True, stop=True,
                     )
-        for t in range(PACK):
-            m = slice(t * P, (t + 1) * P)
-            nc.tensor.matmul_mx(
-                out=h_ps[t][:], lhsT=w3[:, m].bitcast(FP8X4), lhsT_scale=s3[:, m],
-                rhs=b_words[:].bitcast(FP8X4), rhs_scale=b_scales[:], start=True, stop=False,
-            )
+        for u in range(2):
+            cols = slice(u * HALF, (u + 1) * HALF)
+            for t in range(PACK):
+                m = slice(t * P, (t + 1) * P)
+                nc.tensor.matmul_mx(
+                    out=h_ps[u][t // 2][:, t % 2, :], lhsT=w3[:, m].bitcast(FP8X4), lhsT_scale=s32[:, m],
+                    rhs=b_words[:, cols].bitcast(FP8X4), rhs_scale=b_scales[:, cols], start=(t % 2 == 0), stop=False,
+                )
 
         y_win = [sb.tile([P, S], F32, name=f"y_win{t}", align_bytes=64) for t in range(PACK)]
         for t in range(PACK):
             nc.scalar.activation(y_win[t][:], y_ps[t][:], ACT.Copy, scale=gain[:, t : t + 1])
 
+        h_win = [sb.tile([P, S], F32, name=f"h_win{t}", align_bytes=64) for t in range(PACK)]
+        h_sum = [[sb.tile([P, 1], F32, name=f"h_sum{u}_{t}") for t in range(PACK)] for u in range(2)]
+        first_shift = [sb.tile([P, 2], F32, name=f"first_shift{t}") for t in range(PACK)]
+        shift = [sb.tile([P, 2], F32, name=f"shift{t}") for t in range(PACK)]
+
         start = 0
         for c, width in enumerate(Z_CHUNKS):
             cols = slice(start, start + width)
+            u, within = divmod(start, HALF)
             other = [sb.tile([P, width], F32, name=f"other{c}_{t}", align_bytes=64) for t in range(PACK)]
             z_rows = sb.tile([P, PACK, width], BF16, name=f"z_rows{c}", align_bytes=64)
             z_side = sb.tile([P, width * PACK], BF16, name=f"z_side{c}", align_bytes=64)
@@ -148,7 +150,7 @@ def tile_picked_mixindifecn_none_po_kernel(
             z_scales = sb.tile([P, width], U8, name=f"z_scales{c}", align_bytes=64)
             for t in range(PACK):
                 looked_up = y_win[t][:].indirect(entries(n1_t, start, width))
-                if c == 0 and t < 2:
+                if c == 0 and t < 3:
                     nc.vector.tensor_copy(other[t][:], looked_up)
                 else:
                     nc.scalar.activation(other[t][:], looked_up, ACT.Copy)
@@ -157,30 +159,35 @@ def tile_picked_mixindifecn_none_po_kernel(
                     out=z_rows[:, t, :], in0=y_ps[t][:, cols], scalar=gain[:, t : t + 1], in1=other[t][:],
                     op0=ALU.mult, op1=ALU.subtract,
                 )
-            nc.vector.tensor_copy(
-                z_side[:].rearrange("p (c i t) -> p c t i", i=4, t=PACK),
-                z_rows[:].rearrange("p t (c i) -> p c t i", i=4),
-            )
+            side_by_side(nc.scalar.copy if c == 1 else nc.vector.tensor_copy, z_side[:], z_rows[:])
             nc.vector.quantize_mx(out=z_words[:].bitcast(FP8X4), scales=z_scales[:], in_=z_side[:])
+            closes_half = within + width == HALF
             for t in range(PACK):
                 m = slice(t * P, (t + 1) * P)
                 nc.tensor.matmul_mx(
-                    out=h_ps[t][:, cols], lhsT=w2[:, m].bitcast(FP8X4), lhsT_scale=s2[:, m],
-                    rhs=z_words[:].bitcast(FP8X4), rhs_scale=z_scales[:], start=False, stop=(c == len(Z_CHUNKS) - 1),
+                    out=h_ps[u][t // 2][:, t % 2, within : within + width],
+                    lhsT=w2[:, m].bitcast(FP8X4), lhsT_scale=s32[4:P, m],
+                    rhs=z_words[:].bitcast(FP8X4), rhs_scale=z_scales[:], start=False, stop=(closes_half and t % 2 == 1),
                 )
             start += width
 
-        h_win = [sb.tile([P, S], F32, name=f"h_win{t}", align_bytes=64) for t in range(PACK)]
-        h_sum = [sb.tile([P, 1], F32, name=f"h_sum{t}") for t in range(PACK)]
-        shift = [sb.tile([P, 2], F32, name=f"shift{t}") for t in range(PACK)]
-        for t in range(PACK):
-            nc.vector.tensor_scalar(
-                out=h_win[t][:], in0=h_ps[t][:], scalar1=1.0, scalar2=None, op0=ALU.mult, op1=ALU.add,
-                accum_out=h_sum[t][:],
-            )
-            nc.vector.tensor_scalar(
-                out=shift[t][:], in0=coef[:, t, :], scalar1=h_sum[t][:], scalar2=None, op0=ALU.mult,
-            )
+        for u in range(2):
+            for t in range(PACK):
+                half_cols = slice(u * HALF, (u + 1) * HALF)
+                if u == 0:
+                    nc.scalar.activation(h_win[t][:, half_cols], h_ps[u][t // 2][:, t % 2, :], ACT.Copy, accum_out=h_sum[u][t][:])
+                else:
+                    nc.vector.tensor_scalar(
+                        out=h_win[t][:, half_cols], in0=h_ps[u][t // 2][:, t % 2, :], scalar1=1.0, scalar2=None,
+                        op0=ALU.mult, op1=ALU.add, accum_out=h_sum[u][t][:],
+                    )
+                if u == 0:
+                    nc.scalar.activation(first_shift[t][:], coef[:, t, :], ACT.Copy, scale=h_sum[0][t][:])
+                else:
+                    nc.vector.scalar_tensor_tensor(
+                        out=shift[t][:], in0=coef[:, t, :], scalar=h_sum[1][t][:], in1=first_shift[t][:],
+                        op0=ALU.mult, op1=ALU.add,
+                    )
 
         out_rows = out_0.rearrange("(p t) n -> p t n", t=PACK)
         out_words = as_words(out_1)
@@ -198,18 +205,15 @@ def tile_picked_mixindifecn_none_po_kernel(
                     bias=shift[t][:, 0:1], scale=slope[:, t : t + 1],
                 )
                 nc.vector.scalar_tensor_tensor(
-                    out=o_rows[:, t, :], in0=h_ps[t][:, cols], scalar=shift[t][:, 1:2], in1=gate[t][:],
+                    out=o_rows[:, t, :], in0=h_win[t][:, cols], scalar=shift[t][:, 1:2], in1=gate[t][:],
                     op0=ALU.add, op1=ALU.mult,
                 )
             nc.sync.dma_start(out=out_rows[:, :, cols], in_=o_rows[:])
-            nc.vector.tensor_copy(
-                o_side[:].rearrange("p (c i t) -> p c t i", i=4, t=PACK),
-                o_rows[:].rearrange("p t (c i) -> p c t i", i=4),
-            )
+            side_by_side(nc.vector.tensor_copy, o_side[:], o_rows[:])
             nc.vector.quantize_mx(out=o_words[:].bitcast(FP8X4), scales=o_scales[:, cols], in_=o_side[:])
             nc.sync.dma_start(out=out_words[:, cols], in_=o_words[:])
             start += width
         scale_rows = out_2[0].bitcast(I32)
         for q in range(QUADS):
-            queue = nc.scalar if q % 2 else nc.sync
+            queue = nc.sync if q == 0 else nc.scalar
             queue.dma_start(out=scale_rows[4 * q : 4 * q + 4, :], in_=o_scales[32 * q : 32 * q + 4, :].bitcast(I32))

@@ -20,7 +20,7 @@ PACK = 4
 QUADS = 4
 LIST_ROWS = 16
 HALF = S // 2
-Z_CHUNKS = (256, 128, 128)
+Z_CHUNKS = (128, 128, 128, 128)
 OUT_CHUNKS = (256, 128, 128)
 
 
@@ -33,9 +33,9 @@ def tile_picked_mixindifecn_none_po_kernel(
     def as_words(dram):
         return dram[0].rearrange("p n t -> p (n t)").bitcast(I32)
 
-    def load_scale_rows(queues, plane, first_row, dram):
+    def load_scale_rows(plane, first_row, dram, quads):
         rows = dram[0].bitcast(I32)
-        for q, queue in enumerate(queues):
+        for q, queue in quads:
             top = 32 * q + first_row
             queue.dma_start(out=plane[top : top + 4, :].bitcast(I32), in_=rows[4 * q : 4 * q + 4, :])
 
@@ -61,7 +61,7 @@ def tile_picked_mixindifecn_none_po_kernel(
         w1_raw = sb.tile([P, H], I32, name="w1_raw", align_bytes=64)
         w2_raw = sb.tile([P, N], I32, name="w2_raw", align_bytes=64)
         w3_raw = sb.tile([P, N], I32, name="w3_raw", align_bytes=64)
-        s1_raw = sb.tile([P, H], U8, name="s1_raw", tag="s1_then_a", align_bytes=64)
+        s1_raw = sb.tile([P, H], U8, name="s1_raw", align_bytes=64)
         s32_raw = sb.tile([P, N], U8, name="s32_raw", align_bytes=64)
         w1 = sb.tile([P, H], U32, name="w1", align_bytes=64)
         w2 = sb.tile([P, N], U32, name="w2", align_bytes=64)
@@ -73,36 +73,42 @@ def tile_picked_mixindifecn_none_po_kernel(
         coef = sb.tile([P, PACK, 2], F32, name="coef")
 
         nc.vector.memset(xs[:].bitcast(I32), 0)
-        nc.vector.memset(coef[:], -1.0 / S)
         nc.vector.memset(s1_raw[:].bitcast(I32), 0)
+        nc.vector.memset(coef[:], -1.0 / S)
         nc.vector.memset(s32_raw[:].bitcast(I32), 0)
 
         nc.sync.dma_start(offs_t[:], offs)
-        nc.scalar.dma_start(out=slope[:], in_=sl.rearrange("(p t) o -> p (t o)", t=PACK))
         nc.sync.dma_start(two_t[:], two)
-        load_scale_rows([nc.sync] * QUADS, xs, 0, x_scales)
+        load_scale_rows(xs, 0, x_scales, [(q, nc.sync) for q in range(QUADS)])
+        load_scale_rows(s1_raw, 0, w1_scales, [(0, nc.sync)])
         nc.sync.dma_start(out=xw[:], in_=as_words(x_words))
-        load_scale_rows([nc.sync] * QUADS, s1_raw, 0, w1_scales)
+        load_scale_rows(s1_raw, 0, w1_scales, [(1, nc.sync), (2, nc.sync), (3, nc.sync)])
         nc.gpsimd.dma_start(out=gain[:], in_=gn.rearrange("(p t) o -> p (t o)", t=PACK))
         nc.sync.dma_start(out=w1_raw[:], in_=as_words(w1_words))
         nc.sync.dma_start(out=w3_raw[:], in_=as_words(w3_words))
         nc.sync.dma_start(out=w2_raw[:], in_=as_words(w2_words))
-        load_scale_rows([nc.sync] * QUADS, s32_raw, 0, w3_scales)
-        load_scale_rows([nc.sync, nc.sync, nc.gpsimd, nc.gpsimd], s32_raw, 4, w2_scales)
+        load_scale_rows(s32_raw, 0, w3_scales, [(q, nc.sync) for q in range(QUADS)])
         nc.sync.dma_start(n1_t[:], n1)
+        load_scale_rows(s32_raw, 4, w2_scales, [(0, nc.sync), (1, nc.sync), (2, nc.gpsimd), (3, nc.gpsimd)])
         nc.sync.dma_start(n2_t[:], n2)
+        nc.sync.dma_start(out=slope[:], in_=sl.rearrange("(p t) o -> p (t o)", t=PACK))
+        warm = sb.tile([P, 1], F32, name="warm")
+        nc.scalar.activation(warm[:], coef[:, 0, 1:2], ACT.Sigmoid)
 
-        nc.scalar.activation(coef[:, :, 0], slope[:], ACT.Copy, scale=-1.0 / S)
 
         a_scales = sb.tile([P, S], U8, name="a_scales", align_bytes=64)
         b_scales = sb.tile([P, S], U8, name="b_scales", align_bytes=64)
-        picked = sb.tile([P, 2 * S], U32, name="picked", tag="s1_then_a", align_bytes=64)
+        picked = sb.tile([P, 2 * S], U32, name="picked", align_bytes=64)
         a_words = picked[:, 0:S]
         b_words = picked[:, S : 2 * S]
         nc.vector.tensor_copy(a_scales[:], xs[:].indirect(offs_t[:]))
         nc.vector.tensor_copy(b_scales[:], xs[:].indirect(two_t[:]))
-        deal(nc.vector.tensor_copy, s1[:], s1_raw[:])
-        deal(nc.scalar.copy, w1[:], w1_raw[:].bitcast(U32))
+        nc.gpsimd.tensor_copy(s1[:].rearrange("p (t m) -> p t m", t=PACK), s1_raw[:].rearrange("p (m t) -> p t m", t=PACK))
+        for pair in range(2):
+            nc.scalar.copy(
+                w1[:].rearrange("p (t m) -> p m t", t=PACK)[:, :, 2 * pair : 2 * pair + 2],
+                w1_raw[:].bitcast(U32).rearrange("p (m t) -> p m t", t=PACK)[:, :, 2 * pair : 2 * pair + 2],
+            )
         for u in range(2):
             nc.vector.tensor_copy(a_words[:, u * HALF : (u + 1) * HALF], xw[:].bitcast(U32).indirect(entries(offs_t, u * HALF, HALF)))
         deal(nc.scalar.copy, w3[:], w3_raw[:].bitcast(U32))
@@ -112,22 +118,21 @@ def tile_picked_mixindifecn_none_po_kernel(
 
         y_ps = [ps.tile([P, S], F32, name=f"y_ps{t}") for t in range(PACK)]
         h_ps = [[ps.tile([P, 2, HALF], F32, name=f"h_ps{u}_{pair}") for pair in range(2)] for u in range(2)]
-        for pair in range(2):
+        for t in range(PACK):
             for u in range(2):
-                for t in (2 * pair, 2 * pair + 1):
-                    m = slice(t * P, (t + 1) * P)
-                    cols = slice(u * HALF, (u + 1) * HALF)
-                    nc.tensor.matmul_mx(
-                        out=y_ps[t][:, cols], lhsT=w1[:, m].bitcast(FP8X4), lhsT_scale=s1[:, m],
-                        rhs=a_words[:, cols].bitcast(FP8X4), rhs_scale=a_scales[:, cols], start=True, stop=True,
-                    )
+                m = slice(t * P, (t + 1) * P)
+                cols = slice(u * HALF, (u + 1) * HALF)
+                nc.tensor.matmul_mx(
+                    out=y_ps[t][:, cols], lhsT=w1[:, m].bitcast(FP8X4), lhsT_scale=s1[:, m],
+                    rhs=a_words[:, cols].bitcast(FP8X4), rhs_scale=a_scales[:, cols], start=True, stop=True,
+                )
         for u in range(2):
             cols = slice(u * HALF, (u + 1) * HALF)
             for t in range(PACK):
                 m = slice(t * P, (t + 1) * P)
                 nc.tensor.matmul_mx(
-                    out=h_ps[u][t // 2][:, t % 2, :], lhsT=w3[:, m].bitcast(FP8X4), lhsT_scale=s32[:, m],
-                    rhs=b_words[:, cols].bitcast(FP8X4), rhs_scale=b_scales[:, cols], start=(t % 2 == 0), stop=False,
+                    out=h_ps[u][t % 2][:, t // 2, :], lhsT=w3[:, m].bitcast(FP8X4), lhsT_scale=s32[:, m],
+                    rhs=b_words[:, cols].bitcast(FP8X4), rhs_scale=b_scales[:, cols], start=(t < 2), stop=False,
                 )
 
         y_win = [sb.tile([P, S], F32, name=f"y_win{t}", align_bytes=64) for t in range(PACK)]
@@ -139,46 +144,49 @@ def tile_picked_mixindifecn_none_po_kernel(
         first_shift = [sb.tile([P, 2], F32, name=f"first_shift{t}") for t in range(PACK)]
         shift = [sb.tile([P, 2], F32, name=f"shift{t}") for t in range(PACK)]
 
+        others = [[sb.tile([P, width], F32, name=f"other{c}_{t}", align_bytes=64) for t in range(PACK)] for c, width in enumerate(Z_CHUNKS)]
+        on_vector = [(0, 0), (1, 0), (0, 1), (1, 1), (0, 2)]
+        for c, t in on_vector:
+            nc.vector.tensor_copy(others[c][t][:], y_win[t][:].indirect(entries(n1_t, sum(Z_CHUNKS[:c]), Z_CHUNKS[c])))
         start = 0
         for c, width in enumerate(Z_CHUNKS):
             cols = slice(start, start + width)
             u, within = divmod(start, HALF)
-            other = [sb.tile([P, width], F32, name=f"other{c}_{t}", align_bytes=64) for t in range(PACK)]
+            other = others[c]
             z_rows = sb.tile([P, PACK, width], BF16, name=f"z_rows{c}", align_bytes=64)
             z_side = sb.tile([P, width * PACK], BF16, name=f"z_side{c}", align_bytes=64)
             z_words = sb.tile([P, width], U32, name=f"z_words{c}", align_bytes=64)
             z_scales = sb.tile([P, width], U8, name=f"z_scales{c}", align_bytes=64)
             for t in range(PACK):
                 looked_up = y_win[t][:].indirect(entries(n1_t, start, width))
-                if c == 0 and t < 3:
-                    nc.vector.tensor_copy(other[t][:], looked_up)
-                else:
+                if (c, t) not in on_vector:
                     nc.scalar.activation(other[t][:], looked_up, ACT.Copy)
             for t in range(PACK):
                 nc.vector.scalar_tensor_tensor(
                     out=z_rows[:, t, :], in0=y_ps[t][:, cols], scalar=gain[:, t : t + 1], in1=other[t][:],
                     op0=ALU.mult, op1=ALU.subtract,
                 )
-            side_by_side(nc.scalar.copy if c == 1 else nc.vector.tensor_copy, z_side[:], z_rows[:])
+            side_by_side(nc.vector.tensor_copy, z_side[:], z_rows[:])
             nc.vector.quantize_mx(out=z_words[:].bitcast(FP8X4), scales=z_scales[:], in_=z_side[:])
             closes_half = within + width == HALF
-            for t in range(PACK):
+            for t in (0, 2, 1, 3):
                 m = slice(t * P, (t + 1) * P)
                 nc.tensor.matmul_mx(
-                    out=h_ps[u][t // 2][:, t % 2, within : within + width],
+                    out=h_ps[u][t % 2][:, t // 2, within : within + width],
                     lhsT=w2[:, m].bitcast(FP8X4), lhsT_scale=s32[4:P, m],
-                    rhs=z_words[:].bitcast(FP8X4), rhs_scale=z_scales[:], start=False, stop=(closes_half and t % 2 == 1),
+                    rhs=z_words[:].bitcast(FP8X4), rhs_scale=z_scales[:], start=False, stop=(closes_half and t >= 2),
                 )
             start += width
 
+        nc.scalar.activation(coef[:, :, 0], slope[:], ACT.Copy, scale=-1.0 / S)
         for u in range(2):
-            for t in range(PACK):
+            for t in (0, 2, 1, 3):
                 half_cols = slice(u * HALF, (u + 1) * HALF)
-                if u == 0:
-                    nc.scalar.activation(h_win[t][:, half_cols], h_ps[u][t // 2][:, t % 2, :], ACT.Copy, accum_out=h_sum[u][t][:])
+                if u == 0 or t % 2 == 0:
+                    nc.scalar.activation(h_win[t][:, half_cols], h_ps[u][t % 2][:, t // 2, :], ACT.Copy, accum_out=h_sum[u][t][:])
                 else:
                     nc.vector.tensor_scalar(
-                        out=h_win[t][:, half_cols], in0=h_ps[u][t // 2][:, t % 2, :], scalar1=1.0, scalar2=None,
+                        out=h_win[t][:, half_cols], in0=h_ps[u][t % 2][:, t // 2, :], scalar1=1.0, scalar2=None,
                         op0=ALU.mult, op1=ALU.add, accum_out=h_sum[u][t][:],
                     )
                 if u == 0:

@@ -18,10 +18,16 @@ ACT = mybir.ActivationFunctionType
 P = 128
 PACK = 4
 QUADS = 4
+QUAD_ROWS = 4
 LIST_ROWS = 16
+LINE = 4
 HALF = S // 2
-Z_CHUNKS = (128, 128, 128, 128)
-OUT_CHUNKS = (256, 128, 128)
+W2_SCALE_ROW = 4
+Z_WIDTH = 128
+Z_CHUNKS = S // Z_WIDTH
+VECTOR_SETS, VECTOR_CHUNKS = 3, 2
+OUT_WIDTHS = (256, 128, 128)
+BANK_ORDER = (0, 2, 1, 3)
 
 
 def tile_picked_mixindifecn_none_po_kernel(
@@ -33,20 +39,33 @@ def tile_picked_mixindifecn_none_po_kernel(
     def as_words(dram):
         return dram[0].rearrange("p n t -> p (n t)").bitcast(I32)
 
+    def by_row_set(dram):
+        return dram.rearrange("(p t) o -> p (t o)", t=PACK)
+
     def load_scale_rows(plane, first_row, dram, quads):
         rows = dram[0].bitcast(I32)
         for q, queue in quads:
             top = 32 * q + first_row
-            queue.dma_start(out=plane[top : top + 4, :].bitcast(I32), in_=rows[4 * q : 4 * q + 4, :])
+            queue.dma_start(
+                out=plane[top : top + QUAD_ROWS, :].bitcast(I32), in_=rows[QUAD_ROWS * q : QUAD_ROWS * (q + 1), :]
+            )
 
     def entries(lists, start, width):
         return lists[:, start // LIST_ROWS : (start + width) // LIST_ROWS]
 
-    def deal(copy, dst, src):
-        copy(dst.rearrange("p (t m) -> p m t", t=PACK), src.rearrange("p (m t) -> p m t", t=PACK))
+    def dealt(ap):
+        return ap.rearrange("p (t m) -> p m t", t=PACK)
 
-    def side_by_side(copy, dst, src):
-        copy(dst.rearrange("p (c i t) -> p c t i", i=4, t=PACK), src.rearrange("p t (c i) -> p c t i", i=4))
+    def undealt(ap):
+        return ap.rearrange("p (m t) -> p m t", t=PACK)
+
+    def interleave(side, rows):
+        nc.vector.tensor_copy(
+            side.rearrange("p (c i t) -> p c t i", i=LINE, t=PACK), rows.rearrange("p t (c i) -> p c t i", i=LINE)
+        )
+
+    def stationary(t):
+        return slice(t * P, (t + 1) * P)
 
     with ExitStack() as ctx:
         sb = ctx.enter_context(tc.tile_pool(name="sb", bufs=1))
@@ -77,24 +96,25 @@ def tile_picked_mixindifecn_none_po_kernel(
         nc.vector.memset(coef[:], -1.0 / S)
         nc.vector.memset(s32_raw[:].bitcast(I32), 0)
 
+        all_on_sync = [(q, nc.sync) for q in range(QUADS)]
         nc.sync.dma_start(offs_t[:], offs)
         nc.sync.dma_start(two_t[:], two)
-        load_scale_rows(xs, 0, x_scales, [(q, nc.sync) for q in range(QUADS)])
-        load_scale_rows(s1_raw, 0, w1_scales, [(0, nc.sync)])
+        load_scale_rows(xs, 0, x_scales, all_on_sync)
+        load_scale_rows(s1_raw, 0, w1_scales, all_on_sync[:1])
         nc.sync.dma_start(out=xw[:], in_=as_words(x_words))
-        load_scale_rows(s1_raw, 0, w1_scales, [(1, nc.sync), (2, nc.sync), (3, nc.sync)])
-        nc.gpsimd.dma_start(out=gain[:], in_=gn.rearrange("(p t) o -> p (t o)", t=PACK))
+        load_scale_rows(s1_raw, 0, w1_scales, all_on_sync[1:])
+        nc.gpsimd.dma_start(out=gain[:], in_=by_row_set(gn))
         nc.sync.dma_start(out=w1_raw[:], in_=as_words(w1_words))
         nc.sync.dma_start(out=w3_raw[:], in_=as_words(w3_words))
         nc.sync.dma_start(out=w2_raw[:], in_=as_words(w2_words))
-        load_scale_rows(s32_raw, 0, w3_scales, [(q, nc.sync) for q in range(QUADS)])
+        load_scale_rows(s32_raw, 0, w3_scales, all_on_sync)
+        load_scale_rows(s32_raw, W2_SCALE_ROW, w2_scales, all_on_sync[:2] + [(2, nc.gpsimd), (3, nc.gpsimd)])
         nc.sync.dma_start(n1_t[:], n1)
-        load_scale_rows(s32_raw, 4, w2_scales, [(0, nc.sync), (1, nc.sync), (2, nc.gpsimd), (3, nc.gpsimd)])
         nc.sync.dma_start(n2_t[:], n2)
-        nc.sync.dma_start(out=slope[:], in_=sl.rearrange("(p t) o -> p (t o)", t=PACK))
+        nc.sync.dma_start(out=slope[:], in_=by_row_set(sl))
+
         warm = sb.tile([P, 1], F32, name="warm")
         nc.scalar.activation(warm[:], coef[:, 0, 1:2], ACT.Sigmoid)
-
 
         a_scales = sb.tile([P, S], U8, name="a_scales", align_bytes=64)
         b_scales = sb.tile([P, S], U8, name="b_scales", align_bytes=64)
@@ -103,36 +123,37 @@ def tile_picked_mixindifecn_none_po_kernel(
         b_words = picked[:, S : 2 * S]
         nc.vector.tensor_copy(a_scales[:], xs[:].indirect(offs_t[:]))
         nc.vector.tensor_copy(b_scales[:], xs[:].indirect(two_t[:]))
-        nc.gpsimd.tensor_copy(s1[:].rearrange("p (t m) -> p t m", t=PACK), s1_raw[:].rearrange("p (m t) -> p t m", t=PACK))
+        nc.gpsimd.tensor_copy(
+            s1[:].rearrange("p (t m) -> p t m", t=PACK), s1_raw[:].rearrange("p (m t) -> p t m", t=PACK)
+        )
         for pair in range(2):
-            nc.scalar.copy(
-                w1[:].rearrange("p (t m) -> p m t", t=PACK)[:, :, 2 * pair : 2 * pair + 2],
-                w1_raw[:].bitcast(U32).rearrange("p (m t) -> p m t", t=PACK)[:, :, 2 * pair : 2 * pair + 2],
-            )
+            two_sets = slice(2 * pair, 2 * pair + 2)
+            nc.scalar.copy(dealt(w1[:])[:, :, two_sets], undealt(w1_raw[:].bitcast(U32))[:, :, two_sets])
         for u in range(2):
-            nc.vector.tensor_copy(a_words[:, u * HALF : (u + 1) * HALF], xw[:].bitcast(U32).indirect(entries(offs_t, u * HALF, HALF)))
-        deal(nc.scalar.copy, w3[:], w3_raw[:].bitcast(U32))
+            nc.vector.tensor_copy(
+                a_words[:, u * HALF : (u + 1) * HALF], xw[:].bitcast(U32).indirect(entries(offs_t, u * HALF, HALF))
+            )
+        nc.scalar.copy(dealt(w3[:]), undealt(w3_raw[:].bitcast(U32)))
         nc.vector.tensor_copy(b_words, xw[:].bitcast(U32).indirect(two_t[:]))
-        deal(nc.vector.tensor_copy, w2[:].bitcast(I32), w2_raw[:])
-        deal(nc.vector.tensor_copy, s32[:], s32_raw[:])
+        nc.vector.tensor_copy(dealt(w2[:].bitcast(I32)), undealt(w2_raw[:]))
+        nc.vector.tensor_copy(dealt(s32[:]), undealt(s32_raw[:]))
 
         y_ps = [ps.tile([P, S], F32, name=f"y_ps{t}") for t in range(PACK)]
-        h_ps = [[ps.tile([P, 2, HALF], F32, name=f"h_ps{u}_{pair}") for pair in range(2)] for u in range(2)]
+        h_ps = [[ps.tile([P, 2, HALF], F32, name=f"h_ps{u}_{parity}") for parity in range(2)] for u in range(2)]
         for t in range(PACK):
             for u in range(2):
-                m = slice(t * P, (t + 1) * P)
                 cols = slice(u * HALF, (u + 1) * HALF)
                 nc.tensor.matmul_mx(
-                    out=y_ps[t][:, cols], lhsT=w1[:, m].bitcast(FP8X4), lhsT_scale=s1[:, m],
+                    out=y_ps[t][:, cols], lhsT=w1[:, stationary(t)].bitcast(FP8X4), lhsT_scale=s1[:, stationary(t)],
                     rhs=a_words[:, cols].bitcast(FP8X4), rhs_scale=a_scales[:, cols], start=True, stop=True,
                 )
         for u in range(2):
             cols = slice(u * HALF, (u + 1) * HALF)
             for t in range(PACK):
-                m = slice(t * P, (t + 1) * P)
                 nc.tensor.matmul_mx(
-                    out=h_ps[u][t % 2][:, t // 2, :], lhsT=w3[:, m].bitcast(FP8X4), lhsT_scale=s32[:, m],
-                    rhs=b_words[:, cols].bitcast(FP8X4), rhs_scale=b_scales[:, cols], start=(t < 2), stop=False,
+                    out=h_ps[u][t % 2][:, t // 2, :],
+                    lhsT=w3[:, stationary(t)].bitcast(FP8X4), lhsT_scale=s32[:, stationary(t)],
+                    rhs=b_words[:, cols].bitcast(FP8X4), rhs_scale=b_scales[:, cols], start=(t // 2 == 0), stop=False,
                 )
 
         y_win = [sb.tile([P, S], F32, name=f"y_win{t}", align_bytes=64) for t in range(PACK)]
@@ -144,49 +165,51 @@ def tile_picked_mixindifecn_none_po_kernel(
         first_shift = [sb.tile([P, 2], F32, name=f"first_shift{t}") for t in range(PACK)]
         shift = [sb.tile([P, 2], F32, name=f"shift{t}") for t in range(PACK)]
 
-        others = [[sb.tile([P, width], F32, name=f"other{c}_{t}", align_bytes=64) for t in range(PACK)] for c, width in enumerate(Z_CHUNKS)]
-        on_vector = [(0, 0), (1, 0), (0, 1), (1, 1), (0, 2)]
-        for c, t in on_vector:
-            nc.vector.tensor_copy(others[c][t][:], y_win[t][:].indirect(entries(n1_t, sum(Z_CHUNKS[:c]), Z_CHUNKS[c])))
-        start = 0
-        for c, width in enumerate(Z_CHUNKS):
-            cols = slice(start, start + width)
-            u, within = divmod(start, HALF)
-            other = others[c]
-            z_rows = sb.tile([P, PACK, width], BF16, name=f"z_rows{c}", align_bytes=64)
-            z_side = sb.tile([P, width * PACK], BF16, name=f"z_side{c}", align_bytes=64)
-            z_words = sb.tile([P, width], U32, name=f"z_words{c}", align_bytes=64)
-            z_scales = sb.tile([P, width], U8, name=f"z_scales{c}", align_bytes=64)
+        fetched = [
+            [sb.tile([P, Z_WIDTH], F32, name=f"fetched{c}_{t}", align_bytes=64) for t in range(PACK)]
+            for c in range(Z_CHUNKS)
+        ]
+        for t in range(VECTOR_SETS):
+            for c in range(VECTOR_CHUNKS):
+                nc.vector.tensor_copy(fetched[c][t][:], y_win[t][:].indirect(entries(n1_t, c * Z_WIDTH, Z_WIDTH)))
+        for c in range(Z_CHUNKS):
+            cols = slice(c * Z_WIDTH, (c + 1) * Z_WIDTH)
+            u, within = divmod(c * Z_WIDTH, HALF)
+            z_rows = sb.tile([P, PACK, Z_WIDTH], BF16, name=f"z_rows{c}", align_bytes=64)
+            z_side = sb.tile([P, Z_WIDTH * PACK], BF16, name=f"z_side{c}", align_bytes=64)
+            z_words = sb.tile([P, Z_WIDTH], U32, name=f"z_words{c}", align_bytes=64)
+            z_scales = sb.tile([P, Z_WIDTH], U8, name=f"z_scales{c}", align_bytes=64)
             for t in range(PACK):
-                looked_up = y_win[t][:].indirect(entries(n1_t, start, width))
-                if (c, t) not in on_vector:
-                    nc.scalar.activation(other[t][:], looked_up, ACT.Copy)
+                if t >= VECTOR_SETS or c >= VECTOR_CHUNKS:
+                    nc.scalar.activation(
+                        fetched[c][t][:], y_win[t][:].indirect(entries(n1_t, c * Z_WIDTH, Z_WIDTH)), ACT.Copy
+                    )
             for t in range(PACK):
                 nc.vector.scalar_tensor_tensor(
-                    out=z_rows[:, t, :], in0=y_ps[t][:, cols], scalar=gain[:, t : t + 1], in1=other[t][:],
+                    out=z_rows[:, t, :], in0=y_ps[t][:, cols], scalar=gain[:, t : t + 1], in1=fetched[c][t][:],
                     op0=ALU.mult, op1=ALU.subtract,
                 )
-            side_by_side(nc.vector.tensor_copy, z_side[:], z_rows[:])
+            interleave(z_side[:], z_rows[:])
             nc.vector.quantize_mx(out=z_words[:].bitcast(FP8X4), scales=z_scales[:], in_=z_side[:])
-            closes_half = within + width == HALF
-            for t in (0, 2, 1, 3):
-                m = slice(t * P, (t + 1) * P)
+            closes_half = within + Z_WIDTH == HALF
+            for t in BANK_ORDER:
                 nc.tensor.matmul_mx(
-                    out=h_ps[u][t % 2][:, t // 2, within : within + width],
-                    lhsT=w2[:, m].bitcast(FP8X4), lhsT_scale=s32[4:P, m],
-                    rhs=z_words[:].bitcast(FP8X4), rhs_scale=z_scales[:], start=False, stop=(closes_half and t >= 2),
+                    out=h_ps[u][t % 2][:, t // 2, within : within + Z_WIDTH],
+                    lhsT=w2[:, stationary(t)].bitcast(FP8X4), lhsT_scale=s32[W2_SCALE_ROW:P, stationary(t)],
+                    rhs=z_words[:].bitcast(FP8X4), rhs_scale=z_scales[:],
+                    start=False, stop=(closes_half and t // 2 == 1),
                 )
-            start += width
 
         nc.scalar.activation(coef[:, :, 0], slope[:], ACT.Copy, scale=-1.0 / S)
         for u in range(2):
-            for t in (0, 2, 1, 3):
-                half_cols = slice(u * HALF, (u + 1) * HALF)
+            cols = slice(u * HALF, (u + 1) * HALF)
+            for t in BANK_ORDER:
+                bank_part = h_ps[u][t % 2][:, t // 2, :]
                 if u == 0 or t % 2 == 0:
-                    nc.scalar.activation(h_win[t][:, half_cols], h_ps[u][t % 2][:, t // 2, :], ACT.Copy, accum_out=h_sum[u][t][:])
+                    nc.scalar.activation(h_win[t][:, cols], bank_part, ACT.Copy, accum_out=h_sum[u][t][:])
                 else:
                     nc.vector.tensor_scalar(
-                        out=h_win[t][:, half_cols], in0=h_ps[u][t % 2][:, t // 2, :], scalar1=1.0, scalar2=None,
+                        out=h_win[t][:, cols], in0=bank_part, scalar1=1.0, scalar2=None,
                         op0=ALU.mult, op1=ALU.add, accum_out=h_sum[u][t][:],
                     )
                 if u == 0:
@@ -201,7 +224,7 @@ def tile_picked_mixindifecn_none_po_kernel(
         out_words = as_words(out_1)
         o_scales = sb.tile([P, S], U8, name="o_scales", align_bytes=64)
         start = 0
-        for c, width in enumerate(OUT_CHUNKS):
+        for c, width in enumerate(OUT_WIDTHS):
             cols = slice(start, start + width)
             gate = [sb.tile([P, width], F32, name=f"gate{c}_{t}", align_bytes=64) for t in range(PACK)]
             o_rows = sb.tile([P, PACK, width], F32, name=f"o_rows{c}", align_bytes=64)
@@ -217,11 +240,15 @@ def tile_picked_mixindifecn_none_po_kernel(
                     op0=ALU.add, op1=ALU.mult,
                 )
             nc.sync.dma_start(out=out_rows[:, :, cols], in_=o_rows[:])
-            side_by_side(nc.vector.tensor_copy, o_side[:], o_rows[:])
+            interleave(o_side[:], o_rows[:])
             nc.vector.quantize_mx(out=o_words[:].bitcast(FP8X4), scales=o_scales[:, cols], in_=o_side[:])
             nc.sync.dma_start(out=out_words[:, cols], in_=o_words[:])
             start += width
+
         scale_rows = out_2[0].bitcast(I32)
         for q in range(QUADS):
             queue = nc.sync if q == 0 else nc.scalar
-            queue.dma_start(out=scale_rows[4 * q : 4 * q + 4, :], in_=o_scales[32 * q : 32 * q + 4, :].bitcast(I32))
+            queue.dma_start(
+                out=scale_rows[QUAD_ROWS * q : QUAD_ROWS * (q + 1), :],
+                in_=o_scales[32 * q : 32 * q + QUAD_ROWS, :].bitcast(I32),
+            )

from contextlib import ExitStack

import concourse.mybir as mybir

K, T, S, N, H = 512, 2048, 512, 512, 512
FLOPS = 2 * S * (K * H + H * N + K * N)

F32 = mybir.dt.float32
BF16 = mybir.dt.bfloat16
I32 = mybir.dt.int32
U32 = mybir.dt.uint32
U16 = mybir.dt.uint16
U8 = mybir.dt.uint8
FP8X4 = mybir.dt.float8_e4m3fn_x4
ALU = mybir.AluOpType
ACT = mybir.ActivationFunctionType

P = 128
PACK = 4
QUADS = 4
QUAD_ROWS = 4
LIST_ROWS = 16
LINE = 4
HALF = S // 2
W2_SCALE_ROW = 4
Z_WIDTH = 128
Z_CHUNKS = S // Z_WIDTH
VECTOR_SETS, VECTOR_CHUNKS = 3, 2
OUT_WIDTHS = (256, 128, 128)
BANK_ORDER = (0, 2, 1, 3)


def tile_picked_mixindifecn_none_po_kernel(
    tc, x_words, x_scales, w1_words, w1_scales, gn, w2_words, w2_scales, w3_words, w3_scales, sl, offs, n1, two, n2,
    out_0, out_1, out_2,
):
    nc = tc.nc

    def as_words(dram):
        return dram[0].rearrange("p n t -> p (n t)").bitcast(I32)

    def by_row_set(dram):
        return dram.rearrange("(p t) o -> p (t o)", t=PACK)

    def load_scale_rows(plane, first_row, dram, quads):
        rows = dram[0].bitcast(I32)
        for q, queue in quads:
            top = 32 * q + first_row
            queue.dma_start(
                out=plane[top : top + QUAD_ROWS, :].bitcast(I32), in_=rows[QUAD_ROWS * q : QUAD_ROWS * (q + 1), :]
            )

    def entries(lists, start, width):
        return lists[:, start // LIST_ROWS : (start + width) // LIST_ROWS]

    def dealt(ap):
        return ap.rearrange("p (t m) -> p m t", t=PACK)

    def undealt(ap):
        return ap.rearrange("p (m t) -> p m t", t=PACK)

    def interleave(side, rows):
        nc.vector.tensor_copy(
            side.rearrange("p (c i t) -> p c t i", i=LINE, t=PACK), rows.rearrange("p t (c i) -> p c t i", i=LINE)
        )

    def stationary(t):
        return slice(t * P, (t + 1) * P)

    with ExitStack() as ctx:
        sb = ctx.enter_context(tc.tile_pool(name="sb", bufs=1))
        ps = ctx.enter_context(tc.psum_pool(name="ps", bufs=1))

        offs_t = sb.tile([P, S // LIST_ROWS], U16, name="offs_t")
        two_t = sb.tile([P, S // LIST_ROWS], U16, name="two_t")
        n1_t = sb.tile([P, S // LIST_ROWS], U16, name="n1_t")
        n2_t = sb.tile([P, S // LIST_ROWS], U16, name="n2_t")
        xw = sb.tile([P, T], I32, name="xw", align_bytes=64)
        xs = sb.tile([P, T], U8, name="xs", align_bytes=64)
        w1_raw = sb.tile([P, H], I32, name="w1_raw", align_bytes=64)
        w2_raw = sb.tile([P, N], I32, name="w2_raw", align_bytes=64)
        w3_raw = sb.tile([P, N], I32, name="w3_raw", align_bytes=64)
        s1_raw = sb.tile([P, H], U8, name="s1_raw", align_bytes=64)
        s32_raw = sb.tile([P, N], U8, name="s32_raw", align_bytes=64)
        w1 = sb.tile([P, H], U32, name="w1", align_bytes=64)
        w2 = sb.tile([P, N], U32, name="w2", align_bytes=64)
        w3 = sb.tile([P, N], U32, name="w3", align_bytes=64)
        s1 = sb.tile([P, H], U8, name="s1", align_bytes=64)
        s32 = sb.tile([P, N], U8, name="s32", align_bytes=64)
        gain = sb.tile([P, PACK], F32, name="gain")
        slope = sb.tile([P, PACK], F32, name="slope")
        coef = sb.tile([P, PACK, 2], F32, name="coef")

        nc.vector.memset(xs[:].bitcast(I32), 0)
        nc.vector.memset(s1_raw[:].bitcast(I32), 0)
        nc.vector.memset(coef[:], -1.0 / S)
        nc.vector.memset(s32_raw[:].bitcast(I32), 0)

        all_on_sync = [(q, nc.sync) for q in range(QUADS)]
        nc.sync.dma_start(offs_t[:], offs)
        nc.sync.dma_start(two_t[:], two)
        load_scale_rows(xs, 0, x_scales, all_on_sync)
        load_scale_rows(s1_raw, 0, w1_scales, all_on_sync[:1])
        nc.sync.dma_start(out=xw[:], in_=as_words(x_words))
        load_scale_rows(s1_raw, 0, w1_scales, all_on_sync[1:])
        nc.gpsimd.dma_start(out=gain[:], in_=by_row_set(gn))
        nc.sync.dma_start(out=w1_raw[:], in_=as_words(w1_words))
        nc.sync.dma_start(out=w3_raw[:], in_=as_words(w3_words))
        nc.sync.dma_start(out=w2_raw[:], in_=as_words(w2_words))
        load_scale_rows(s32_raw, 0, w3_scales, all_on_sync)
        load_scale_rows(s32_raw, W2_SCALE_ROW, w2_scales, all_on_sync[:2] + [(2, nc.gpsimd), (3, nc.gpsimd)])
        nc.sync.dma_start(n1_t[:], n1)
        nc.sync.dma_start(n2_t[:], n2)
        nc.sync.dma_start(out=slope[:], in_=by_row_set(sl))

        warm = sb.tile([P, 1], F32, name="warm")
        nc.scalar.activation(warm[:], coef[:, 0, 1:2], ACT.Sigmoid)

        a_scales = sb.tile([P, S], U8, name="a_scales", align_bytes=64)
        b_scales = sb.tile([P, S], U8, name="b_scales", align_bytes=64)
        picked = sb.tile([P, 2 * S], U32, name="picked", align_bytes=64)
        a_words = picked[:, 0:S]
        b_words = picked[:, S : 2 * S]
        nc.vector.tensor_copy(a_scales[:], xs[:].indirect(offs_t[:]))
        nc.vector.tensor_copy(b_scales[:], xs[:].indirect(two_t[:]))
        nc.gpsimd.tensor_copy(
            s1[:].rearrange("p (t m) -> p t m", t=PACK), s1_raw[:].rearrange("p (m t) -> p t m", t=PACK)
        )
        for pair in range(2):
            two_sets = slice(2 * pair, 2 * pair + 2)
            nc.scalar.copy(dealt(w1[:])[:, :, two_sets], undealt(w1_raw[:].bitcast(U32))[:, :, two_sets])
        for u in range(2):
            nc.vector.tensor_copy(
                a_words[:, u * HALF : (u + 1) * HALF], xw[:].bitcast(U32).indirect(entries(offs_t, u * HALF, HALF))
            )
        nc.scalar.copy(dealt(w3[:]), undealt(w3_raw[:].bitcast(U32)))
        nc.vector.tensor_copy(b_words, xw[:].bitcast(U32).indirect(two_t[:]))
        nc.vector.tensor_copy(dealt(w2[:].bitcast(I32)), undealt(w2_raw[:]))
        nc.vector.tensor_copy(dealt(s32[:]), undealt(s32_raw[:]))

        y_ps = [ps.tile([P, S], F32, name=f"y_ps{t}") for t in range(PACK)]
        h_ps = [[ps.tile([P, 2, HALF], F32, name=f"h_ps{u}_{parity}") for parity in range(2)] for u in range(2)]
        for t in range(PACK):
            for u in range(2):
                cols = slice(u * HALF, (u + 1) * HALF)
                nc.tensor.matmul_mx(
                    out=y_ps[t][:, cols], lhsT=w1[:, stationary(t)].bitcast(FP8X4), lhsT_scale=s1[:, stationary(t)],
                    rhs=a_words[:, cols].bitcast(FP8X4), rhs_scale=a_scales[:, cols], start=True, stop=True,
                )
        for u in range(2):
            cols = slice(u * HALF, (u + 1) * HALF)
            for t in range(PACK):
                nc.tensor.matmul_mx(
                    out=h_ps[u][t % 2][:, t // 2, :],
                    lhsT=w3[:, stationary(t)].bitcast(FP8X4), lhsT_scale=s32[:, stationary(t)],
                    rhs=b_words[:, cols].bitcast(FP8X4), rhs_scale=b_scales[:, cols], start=(t // 2 == 0), stop=False,
                )

        y_win = [sb.tile([P, S], F32, name=f"y_win{t}", align_bytes=64) for t in range(PACK)]
        for t in range(PACK):
            nc.scalar.activation(y_win[t][:], y_ps[t][:], ACT.Copy, scale=gain[:, t : t + 1])

        h_win = [sb.tile([P, S], F32, name=f"h_win{t}", align_bytes=64) for t in range(PACK)]
        h_sum = [[sb.tile([P, 1], F32, name=f"h_sum{u}_{t}") for t in range(PACK)] for u in range(2)]
        first_shift = [sb.tile([P, 2], F32, name=f"first_shift{t}") for t in range(PACK)]
        shift = [sb.tile([P, 2], F32, name=f"shift{t}") for t in range(PACK)]

        fetched = [
            [sb.tile([P, Z_WIDTH], F32, name=f"fetched{c}_{t}", align_bytes=64) for t in range(PACK)]
            for c in range(Z_CHUNKS)
        ]
        for t in range(VECTOR_SETS):
            for c in range(VECTOR_CHUNKS):
                nc.vector.tensor_copy(fetched[c][t][:], y_win[t][:].indirect(entries(n1_t, c * Z_WIDTH, Z_WIDTH)))
        for c in range(Z_CHUNKS):
            cols = slice(c * Z_WIDTH, (c + 1) * Z_WIDTH)
            u, within = divmod(c * Z_WIDTH, HALF)
            z_rows = sb.tile([P, PACK, Z_WIDTH], BF16, name=f"z_rows{c}", align_bytes=64)
            z_side = sb.tile([P, Z_WIDTH * PACK], BF16, name=f"z_side{c}", align_bytes=64)
            z_words = sb.tile([P, Z_WIDTH], U32, name=f"z_words{c}", align_bytes=64)
            z_scales = sb.tile([P, Z_WIDTH], U8, name=f"z_scales{c}", align_bytes=64)
            for t in range(PACK):
                if t >= VECTOR_SETS or c >= VECTOR_CHUNKS:
                    nc.scalar.activation(
                        fetched[c][t][:], y_win[t][:].indirect(entries(n1_t, c * Z_WIDTH, Z_WIDTH)), ACT.Copy
                    )
            for t in range(PACK):
                nc.vector.scalar_tensor_tensor(
                    out=z_rows[:, t, :], in0=y_ps[t][:, cols], scalar=gain[:, t : t + 1], in1=fetched[c][t][:],
                    op0=ALU.mult, op1=ALU.subtract,
                )
            interleave(z_side[:], z_rows[:])
            nc.vector.quantize_mx(out=z_words[:].bitcast(FP8X4), scales=z_scales[:], in_=z_side[:])
            closes_half = within + Z_WIDTH == HALF
            for t in BANK_ORDER:
                nc.tensor.matmul_mx(
                    out=h_ps[u][t % 2][:, t // 2, within : within + Z_WIDTH],
                    lhsT=w2[:, stationary(t)].bitcast(FP8X4), lhsT_scale=s32[W2_SCALE_ROW:P, stationary(t)],
                    rhs=z_words[:].bitcast(FP8X4), rhs_scale=z_scales[:],
                    start=False, stop=(closes_half and t // 2 == 1),
                )

        nc.scalar.activation(coef[:, :, 0], slope[:], ACT.Copy, scale=-1.0 / S)
        for u in range(2):
            cols = slice(u * HALF, (u + 1) * HALF)
            for t in BANK_ORDER:
                bank_part = h_ps[u][t % 2][:, t // 2, :]
                if u == 0 or t % 2 == 0:
                    nc.scalar.activation(h_win[t][:, cols], bank_part, ACT.Copy, accum_out=h_sum[u][t][:])
                else:
                    nc.vector.tensor_scalar(
                        out=h_win[t][:, cols], in0=bank_part, scalar1=1.0, scalar2=None,
                        op0=ALU.mult, op1=ALU.add, accum_out=h_sum[u][t][:],
                    )
                if u == 0:
                    nc.scalar.activation(first_shift[t][:], coef[:, t, :], ACT.Copy, scale=h_sum[0][t][:])
                else:
                    nc.vector.scalar_tensor_tensor(
                        out=shift[t][:], in0=coef[:, t, :], scalar=h_sum[1][t][:], in1=first_shift[t][:],
                        op0=ALU.mult, op1=ALU.add,
                    )

        out_rows = out_0.rearrange("(p t) n -> p t n", t=PACK)
        out_words = as_words(out_1)
        o_scales = sb.tile([P, S], U8, name="o_scales", align_bytes=64)
        start = 0
        for c, width in enumerate(OUT_WIDTHS):
            cols = slice(start, start + width)
            gate = [sb.tile([P, width], F32, name=f"gate{c}_{t}", align_bytes=64) for t in range(PACK)]
            o_rows = sb.tile([P, PACK, width], F32, name=f"o_rows{c}", align_bytes=64)
            o_side = sb.tile([P, width * PACK], BF16, name=f"o_side{c}", align_bytes=64)
            o_words = sb.tile([P, width], I32, name=f"o_words{c}", align_bytes=64)
            for t in range(PACK):
                nc.scalar.activation(
                    gate[t][:], h_win[t][:].indirect(entries(n2_t, start, width)), ACT.Sigmoid,
                    bias=shift[t][:, 0:1], scale=slope[:, t : t + 1],
                )
                nc.vector.scalar_tensor_tensor(
                    out=o_rows[:, t, :], in0=h_win[t][:, cols], scalar=shift[t][:, 1:2], in1=gate[t][:],
                    op0=ALU.add, op1=ALU.mult,
                )
            nc.sync.dma_start(out=out_rows[:, :, cols], in_=o_rows[:])
            interleave(o_side[:], o_rows[:])
            nc.vector.quantize_mx(out=o_words[:].bitcast(FP8X4), scales=o_scales[:, cols], in_=o_side[:])
            nc.sync.dma_start(out=out_words[:, cols], in_=o_words[:])
            start += width

        scale_rows = out_2[0].bitcast(I32)
        for q in range(QUADS):
            queue = nc.sync if q == 0 else nc.scalar
            queue.dma_start(
                out=scale_rows[QUAD_ROWS * q : QUAD_ROWS * (q + 1), :],
                in_=o_scales[32 * q : 32 * q + QUAD_ROWS, :].bitcast(I32),
            )
